import numpy as np
import ml_dtypes


def mxq(x, axis, fmt="e4m3"):
    dtype, down = {"e4m3": (ml_dtypes.float8_e4m3fn, 7), "e5m2": (ml_dtypes.float8_e5m2, 14)}[fmt]
    v = np.moveaxis(np.asarray(x, np.float32).astype(ml_dtypes.bfloat16).astype(np.float64), axis, -1)
    blocks = v.reshape(v.shape[:-1] + (-1, 32))
    amax = np.abs(blocks).max(-1, keepdims=True)
    byte = np.maximum(np.where(amax > 0, np.frexp(amax)[1] - 1 + 127, 0) - down, 1)
    scale = np.exp2(byte - 127.0)
    codes = (blocks / scale).astype(np.float32).astype(dtype).astype(np.float64)
    return np.moveaxis((codes * scale).reshape(v.shape), -1, axis)


WIDE = False


def mx_kscale(k):
    if not WIDE:
        return np.ones(k)
    levels = np.array([10, -10, 5, -5, 0])
    if k % 512:
        return np.exp2(np.random.permutation(np.resize(levels, k // 32))).repeat(32)
    a = np.empty((k // 512, 16))
    for p in range(k // 512):
        a[p, :8] = np.random.permutation(np.resize(levels, 8))
        for g in range(8):
            far = levels[np.abs(levels - a[p, g]) >= 10]
            a[p, g + 8] = far[np.random.randint(len(far))]
    return np.exp2(a.ravel()).repeat(32)


def f64(x):
    return np.asarray(x).astype(np.float64)


def striped(idx):
    return np.tile(idx.reshape(-1, 16).T, (8, 1)).astype(np.uint16)


def unstriped(offs):
    return offs[:16].T.reshape(-1).astype(np.int64)


E2M1 = np.array([0.0, 0.5, 1.0, 1.5, 2.0, 3.0, 4.0, 6.0, -0.0, -0.5, -1.0, -1.5, -2.0, -3.0, -4.0, -6.0])


def pack_weight(w, fmt):
    k, n = w.shape
    w = f64(np.asarray(w, np.float32).astype(ml_dtypes.bfloat16)).reshape(k // 32, 32, n)
    amax = np.abs(w).max(1)
    if fmt == "e4m3":
        byte = np.frexp(amax)[1] - 1 + 127 - 7
    else:
        mant, ex = np.frexp(amax / 6.0)
        byte = np.where(mant > 0.5, ex, ex - 1) + 127
    byte = np.clip(np.where(amax > 0, byte, 1), 1, 254)
    scaled = (w * np.exp2(127.0 - byte)[:, None, :]).reshape(k, n).astype(np.float32)
    by_word = np.ascontiguousarray(scaled.reshape(k // 512, 128, 4, n).transpose(0, 1, 3, 2))
    if fmt == "e4m3":
        words = by_word.astype(ml_dtypes.float8_e4m3fn).view(np.uint8)
    else:
        c = by_word.astype(ml_dtypes.float4_e2m1fn).view(np.uint8) & 0xF
        words = (c[..., 0::2] | (c[..., 1::2] << 4)).reshape(k // 512, 128, 2 * n)
    return np.ascontiguousarray(words), np.ascontiguousarray(byte.astype(np.uint8).reshape(k // 512, 16, n))


def unpack_weight(words, scales, fmt):
    g, _, n = scales.shape
    words = np.ascontiguousarray(words).reshape(g, 128, n, -1)
    if fmt == "e4m3":
        vals = words.view(ml_dtypes.float8_e4m3fn).astype(np.float64)
    else:
        nib = np.empty((g, 128, n, 4), np.uint8)
        nib[..., 0::2] = words & 0xF
        nib[..., 1::2] = words >> 4
        vals = E2M1[nib]
    vals = vals * np.repeat(np.exp2(scales.astype(np.float64) - 127.0), 8, axis=1)[..., None]
    return vals.transpose(0, 1, 3, 2).reshape(g * 512, n)


def gelu(v):
    return 0.5 * v * (1.0 + np.tanh(np.sqrt(2.0 / np.pi) * (v + 0.044715 * v**3)))


K, M, T, S = 512, 512, 4096, 2048


def setup_inputs():
    n = np.random.standard_normal
    s = mx_kscale(K)[:, None]
    s2 = mx_kscale(512)[:, None]
    v = pack_weight(n((K, T)) * s, "e4m3")
    p_w4 = pack_weight(n((K, M)) / np.sqrt(K) / s, "e2m1")
    return {
        "tab_words": v[0],
        "tab_scales": v[1],
        "w4_words": p_w4[0],
        "w4_scales": p_w4[1],
        "c": (n((512, S)) * s2).astype(np.float32),
        "u": (n((512, M)) / np.sqrt(512) / s2).astype(np.float32),
        "gT": n((M, T)).astype(np.float32),
        "b": (0.3 * n(512)).astype(np.float32),
        "offs": striped(np.random.permutation(T)[:S]),
    }


def reference(tab_words, tab_scales, w4_words, w4_scales, c, u, gT, b, offs):
    tab_ = unpack_weight(tab_words, tab_scales, "e4m3")[:, unstriped(offs)]
    w4_ = unpack_weight(w4_words, w4_scales, "e2m1")
    c_ = mxq(f64(c), 0, "e4m3")
    u_ = mxq(f64(u), 0, "e4m3")
    y = w4_.T @ tab_ + u_.T @ c_
    return (gelu(y + f64(b)[:, None])) * f64(gT)[:, unstriped(offs)]

@@ -1,0 +1,158 @@
+from contextlib import ExitStack
+
+import concourse.mybir as mybir
+
+K, M, T, S = 512, 512, 4096, 2048
+FLOPS = 2 * 2 * K * M * S
+
+F32 = mybir.dt.float32
+BF16 = mybir.dt.bfloat16
+I32 = mybir.dt.int32
+U32 = mybir.dt.uint32
+U16 = mybir.dt.uint16
+U8 = mybir.dt.uint8
+FP8X4 = mybir.dt.float8_e4m3fn_x4
+FP4X4 = mybir.dt.float4_e2m1fn_x4
+GELU = mybir.ActivationFunctionType.Gelu_apprx_tanh
+MULT = mybir.AluOpType.mult
+
+P = 128
+PACK = 4
+NT = 512
+CHUNKS = S // NT
+BLOCKS = M // P
+LIST_COLS = NT // 16
+C_LOAD = 1024
+
+
+def load_scale_rows(nc, plane, rows):
+    for q in range(4):
+        nc.sync.dma_start(out=plane[32 * q : 32 * q + 4, :].bitcast(I32), in_=rows[4 * q : 4 * q + 4, :].bitcast(I32))
+
+
+def interleave(copy, grouped, raw):
+    copy(
+        out=grouped[:].rearrange("p (c i) t -> p c t i", i=4),
+        in_=raw.rearrange("p t (c i) -> p c t i", i=4),
+    )
+
+
+def tile_list_tabgate_gelu_kernel(
+    tc, tab_words, tab_scales, w4_words, w4_scales, c, u, gT, b, offs, out
+):
+    nc = tc.nc
+    with ExitStack() as ctx:
+        keep = ctx.enter_context(tc.tile_pool(name="keep", bufs=1))
+        ring = ctx.enter_context(tc.tile_pool(name="ring", bufs=3))
+        psum = ctx.enter_context(tc.psum_pool(name="psum", bufs=8))
+
+        offsets = keep.tile([P, S // 16], U16, name="offsets")
+        u_raw = keep.tile([P, PACK, M], F32, name="u_raw")
+        tab_plane = keep.tile([P, T], U8, name="tab_plane", align_bytes=64)
+        tab_codes = keep.tile([P, T], I32, name="tab_codes", align_bytes=64)
+        c_raw = [keep.tile([P, PACK, C_LOAD], F32, name="c_raw%d" % h) for h in range(S // C_LOAD)]
+        w4_codes = keep.tile([P, 2 * M], U8, name="w4_codes", align_bytes=64)
+        w4_plane = keep.tile([P, M], U8, name="w4_plane", align_bytes=64)
+        b_rows = keep.tile([P, P], F32, name="b_rows", align_bytes=64)
+        b_cols = keep.tile([P, P], F32, name="b_cols", align_bytes=64)
+        gates = [keep.tile([P, T], F32, name="gates%d" % m) for m in range(BLOCKS)]
+
+        nc.vector.memset(tab_plane[:].bitcast(I32), 0)
+        nc.vector.memset(w4_plane[:].bitcast(I32), 0)
+        nc.vector.memset(b_rows[:], 0.0)
+
+        c_view = c.rearrange("(p t) j -> p t j", t=PACK)
+        nc.sync.dma_start(offsets[:], offs)
+        nc.sync.dma_start(out=u_raw[:], in_=u.rearrange("(p t) n -> p t n", t=PACK))
+        load_scale_rows(nc, tab_plane, tab_scales[0])
+        nc.sync.dma_start(
+            out=b_rows[0:P:32, :].rearrange("q (m r) -> q m r", r=32),
+            in_=b.rearrange("(m q r) -> q m r", q=4, r=32),
+        )
+        nc.sync.dma_start(out=c_raw[0][:], in_=c_view[:, :, 0:C_LOAD])
+        nc.sync.dma_start(out=tab_codes[:], in_=tab_words[0].rearrange("p t i -> p (t i)").bitcast(I32))
+        nc.sync.dma_start(out=w4_codes[:].bitcast(I32), in_=w4_words[0].bitcast(I32))
+        load_scale_rows(nc, w4_plane, w4_scales[0])
+        nc.sync.dma_start(out=c_raw[1][:], in_=c_view[:, :, C_LOAD : 2 * C_LOAD])
+        for m in range(BLOCKS):
+            nc.sync.dma_start(out=gates[m][:], in_=gT[m * P : (m + 1) * P, :])
+
+        lists = [offsets[:, j * LIST_COLS : (j + 1) * LIST_COLS] for j in range(CHUNKS)]
+
+        u_grouped = ring.tile([P, M, PACK], BF16, name="grouped", align_bytes=64)
+        interleave(nc.scalar.copy, u_grouped, u_raw[:])
+
+        v_plane = [keep.tile([P, NT], U8, name="v_plane%d" % j, align_bytes=64) for j in range(CHUNKS)]
+        v_codes = [keep.tile([P, NT], U32, name="v_codes%d" % j, align_bytes=64) for j in range(CHUNKS)]
+        for j in range(CHUNKS):
+            nc.vector.tensor_copy(v_plane[j][:], tab_plane[:].indirect(lists[j]))
+
+        u_codes = keep.tile([P, M], U32, name="u_codes", align_bytes=64)
+        u_plane = keep.tile([P, M], U8, name="u_plane", align_bytes=64)
+        nc.vector.quantize_mx(
+            out=u_codes[:].bitcast(FP8X4), scales=u_plane[:], in_=u_grouped[:].rearrange("p w t -> p (w t)")
+        )
+        nc.vector.transpose(b_cols[:], b_rows[:])
+
+        acts = [keep.tile([P, S], F32, name="acts%d" % m, tag="slot%d" % (m + 1), align_bytes=64) for m in range(BLOCKS)]
+        per_load = C_LOAD // NT
+        for half in range(S // C_LOAD):
+            quantised = []
+            for j in range(half * per_load, (half + 1) * per_load):
+                first = j * NT - half * C_LOAD
+                if j == CHUNKS - 1:
+                    c_grouped = keep.tile([P, NT, PACK], BF16, name="last_grouped", tag="slot0", align_bytes=64)
+                else:
+                    c_grouped = ring.tile([P, NT, PACK], BF16, name="grouped", align_bytes=64)
+                copy = nc.scalar.copy if half == 0 else nc.vector.tensor_copy
+                interleave(copy, c_grouped, c_raw[half][:, :, first : first + NT])
+                quantised.append((j, c_grouped))
+            operands = []
+            for j, c_grouped in quantised:
+                c_codes = keep.tile([P, NT], U32, name="c_codes%d" % j, align_bytes=64)
+                c_plane = keep.tile([P, NT], U8, name="c_plane%d" % j, align_bytes=64)
+                nc.vector.quantize_mx(
+                    out=c_codes[:].bitcast(FP8X4), scales=c_plane[:], in_=c_grouped[:].rearrange("p w t -> p (w t)")
+                )
+                operands.append((j, c_codes, c_plane))
+            if half == 0:
+                for j in range(CHUNKS):
+                    nc.vector.tensor_copy(v_codes[j][:], tab_codes[:].bitcast(U32).indirect(lists[j]))
+            for m in range(BLOCKS):
+                rows = slice(m * P, (m + 1) * P)
+                for j, c_codes, c_plane in operands:
+                    acc = psum.tile([P, NT], F32, name="acc")
+                    nc.tensor.matmul_mx(
+                        out=acc[:],
+                        lhsT=w4_codes[:, 2 * m * P : 2 * (m + 1) * P].bitcast(FP4X4),
+                        lhsT_scale=w4_plane[:, rows],
+                        rhs=v_codes[j][:].bitcast(FP8X4),
+                        rhs_scale=v_plane[j][:],
+                        start=True,
+                        stop=False,
+                    )
+                    nc.tensor.matmul_mx(
+                        out=acc[:],
+                        lhsT=u_codes[:, rows].bitcast(FP8X4),
+                        lhsT_scale=u_plane[:, rows],
+                        rhs=c_codes[:].bitcast(FP8X4),
+                        rhs_scale=c_plane[:],
+                        start=False,
+                        stop=True,
+                    )
+                    nc.scalar.activation(
+                        acts[m][:, j * NT : (j + 1) * NT], acc[:], GELU, bias=b_cols[:, 32 * m : 32 * m + 1]
+                    )
+
+        for m in range(BLOCKS):
+            result = keep.tile([P, S], F32, name="result%d" % m, tag="slot%d" % m, align_bytes=64)
+            store_cols = S // 2 if m == BLOCKS - 1 else S
+            for j in range(CHUNKS):
+                cols = slice(j * NT, (j + 1) * NT)
+                nc.vector.tensor_tensor(result[:, cols], gates[m][:].indirect(lists[j]), acts[m][:, cols], MULT)
+                done = (j + 1) * NT
+                if done % store_cols == 0:
+                    nc.sync.dma_start(
+                        out=out[m * P : (m + 1) * P, done - store_cols : done],
+                        in_=result[:, done - store_cols : done],
+                    )

@@ -22,7 +22,7 @@ NT = 512
 CHUNKS = S // NT
 BLOCKS = M // P
 LIST_COLS = NT // 16
-C_LOAD = 1024
+EARLY = 2
 
 
 def load_scale_rows(nc, plane, rows):
@@ -48,9 +48,9 @@ def tile_list_tabgate_gelu_kernel(
 
         offsets = keep.tile([P, S // 16], U16, name="offsets")
         u_raw = keep.tile([P, PACK, M], F32, name="u_raw")
-        tab_plane = keep.tile([P, T], U8, name="tab_plane", align_bytes=64)
+        tab_plane = keep.tile([P, T], U8, name="tab_plane", tag="plane_then_u", align_bytes=64)
         tab_codes = keep.tile([P, T], I32, name="tab_codes", align_bytes=64)
-        c_raw = [keep.tile([P, PACK, C_LOAD], F32, name="c_raw%d" % h) for h in range(S // C_LOAD)]
+        c_raw = [keep.tile([P, PACK, NT], F32, name="c_raw%d" % j) for j in range(CHUNKS)]
         w4_codes = keep.tile([P, 2 * M], U8, name="w4_codes", align_bytes=64)
         w4_plane = keep.tile([P, M], U8, name="w4_plane", align_bytes=64)
         b_rows = keep.tile([P, P], F32, name="b_rows", align_bytes=64)
@@ -62,97 +62,129 @@ def tile_list_tabgate_gelu_kernel(
         nc.vector.memset(b_rows[:], 0.0)
 
         c_view = c.rearrange("(p t) j -> p t j", t=PACK)
+
+        def load_c(j):
+            nc.sync.dma_start(out=c_raw[j][:], in_=c_view[:, :, j * NT : (j + 1) * NT])
+
+        def load_gates(m):
+            nc.sync.dma_start(out=gates[m][:], in_=gT[m * P : (m + 1) * P, :])
+
         nc.sync.dma_start(offsets[:], offs)
+        nc.sync.dma_start(out=w4_codes[:].bitcast(I32), in_=w4_words[0].bitcast(I32))
         nc.sync.dma_start(out=u_raw[:], in_=u.rearrange("(p t) n -> p t n", t=PACK))
         load_scale_rows(nc, tab_plane, tab_scales[0])
+        nc.sync.dma_start(out=tab_codes[:], in_=tab_words[0].rearrange("p t i -> p (t i)").bitcast(I32))
+        load_gates(0)
+        load_scale_rows(nc, w4_plane, w4_scales[0])
         nc.sync.dma_start(
             out=b_rows[0:P:32, :].rearrange("q (m r) -> q m r", r=32),
             in_=b.rearrange("(m q r) -> q m r", q=4, r=32),
         )
-        nc.sync.dma_start(out=c_raw[0][:], in_=c_view[:, :, 0:C_LOAD])
-        nc.sync.dma_start(out=tab_codes[:], in_=tab_words[0].rearrange("p t i -> p (t i)").bitcast(I32))
-        nc.sync.dma_start(out=w4_codes[:].bitcast(I32), in_=w4_words[0].bitcast(I32))
-        load_scale_rows(nc, w4_plane, w4_scales[0])
-        nc.sync.dma_start(out=c_raw[1][:], in_=c_view[:, :, C_LOAD : 2 * C_LOAD])
-        for m in range(BLOCKS):
-            nc.sync.dma_start(out=gates[m][:], in_=gT[m * P : (m + 1) * P, :])
+        load_c(0)
+        load_gates(1)
+        load_c(1)
+        load_c(2)
+        load_gates(2)
+        load_c(3)
+        load_gates(3)
 
-        lists = [offsets[:, j * LIST_COLS : (j + 1) * LIST_COLS] for j in range(CHUNKS)]
+        v_plane = keep.tile([P, S], U8, name="v_plane", align_bytes=64)
+        v_codes = keep.tile([P, S], U32, name="v_codes", align_bytes=64)
+        nc.vector.tensor_copy(v_plane[:], tab_plane[:].indirect(offsets[:]))
+        nc.vector.tensor_copy(v_codes[:], tab_codes[:].bitcast(U32).indirect(offsets[:]))
+        picked = [keep.tile([P, S], F32, name="picked%d" % m) for m in range(EARLY)]
+        nc.vector.tensor_copy(picked[0][:], gates[0][:].indirect(offsets[:]))
 
-        u_grouped = ring.tile([P, M, PACK], BF16, name="grouped", align_bytes=64)
-        interleave(nc.scalar.copy, u_grouped, u_raw[:])
+        def quantise(raw, name, grouped, tag):
+            interleave(nc.scalar.copy, grouped, raw[:])
+            codes = keep.tile([P, NT], U32, name=name + "_codes", tag=tag, align_bytes=64)
+            plane = keep.tile([P, NT], U8, name=name + "_plane", align_bytes=64)
+            nc.vector.quantize_mx(
+                out=codes[:].bitcast(FP8X4), scales=plane[:], in_=grouped[:].rearrange("p w t -> p (w t)")
+            )
+            return codes, plane
 
-        v_plane = [keep.tile([P, NT], U8, name="v_plane%d" % j, align_bytes=64) for j in range(CHUNKS)]
-        v_codes = [keep.tile([P, NT], U32, name="v_codes%d" % j, align_bytes=64) for j in range(CHUNKS)]
-        for j in range(CHUNKS):
-            nc.vector.tensor_copy(v_plane[j][:], tab_plane[:].indirect(lists[j]))
-
-        u_codes = keep.tile([P, M], U32, name="u_codes", align_bytes=64)
-        u_plane = keep.tile([P, M], U8, name="u_plane", align_bytes=64)
-        nc.vector.quantize_mx(
-            out=u_codes[:].bitcast(FP8X4), scales=u_plane[:], in_=u_grouped[:].rearrange("p w t -> p (w t)")
-        )
+        u_codes, u_plane = quantise(u_raw, "u", ring.tile([P, M, PACK], BF16, name="grouped", align_bytes=64), "plane_then_u")
         nc.vector.transpose(b_cols[:], b_rows[:])
 
-        acts = [keep.tile([P, S], F32, name="acts%d" % m, tag="slot%d" % (m + 1), align_bytes=64) for m in range(BLOCKS)]
-        per_load = C_LOAD // NT
-        for half in range(S // C_LOAD):
-            quantised = []
-            for j in range(half * per_load, (half + 1) * per_load):
-                first = j * NT - half * C_LOAD
-                if j == CHUNKS - 1:
-                    c_grouped = keep.tile([P, NT, PACK], BF16, name="last_grouped", tag="slot0", align_bytes=64)
-                else:
-                    c_grouped = ring.tile([P, NT, PACK], BF16, name="grouped", align_bytes=64)
-                copy = nc.scalar.copy if half == 0 else nc.vector.tensor_copy
-                interleave(copy, c_grouped, c_raw[half][:, :, first : first + NT])
-                quantised.append((j, c_grouped))
-            operands = []
-            for j, c_grouped in quantised:
-                c_codes = keep.tile([P, NT], U32, name="c_codes%d" % j, align_bytes=64)
-                c_plane = keep.tile([P, NT], U8, name="c_plane%d" % j, align_bytes=64)
-                nc.vector.quantize_mx(
-                    out=c_codes[:].bitcast(FP8X4), scales=c_plane[:], in_=c_grouped[:].rearrange("p w t -> p (w t)")
-                )
-                operands.append((j, c_codes, c_plane))
-            if half == 0:
-                for j in range(CHUNKS):
-                    nc.vector.tensor_copy(v_codes[j][:], tab_codes[:].bitcast(U32).indirect(lists[j]))
-            for m in range(BLOCKS):
-                rows = slice(m * P, (m + 1) * P)
-                for j, c_codes, c_plane in operands:
-                    acc = psum.tile([P, NT], F32, name="acc")
-                    nc.tensor.matmul_mx(
-                        out=acc[:],
-                        lhsT=w4_codes[:, 2 * m * P : 2 * (m + 1) * P].bitcast(FP4X4),
-                        lhsT_scale=w4_plane[:, rows],
-                        rhs=v_codes[j][:].bitcast(FP8X4),
-                        rhs_scale=v_plane[j][:],
-                        start=True,
-                        stop=False,
-                    )
-                    nc.tensor.matmul_mx(
-                        out=acc[:],
-                        lhsT=u_codes[:, rows].bitcast(FP8X4),
-                        lhsT_scale=u_plane[:, rows],
-                        rhs=c_codes[:].bitcast(FP8X4),
-                        rhs_scale=c_plane[:],
-                        start=False,
-                        stop=True,
-                    )
-                    nc.scalar.activation(
-                        acts[m][:, j * NT : (j + 1) * NT], acc[:], GELU, bias=b_cols[:, 32 * m : 32 * m + 1]
-                    )
+        acts = [keep.tile([P, S], F32, name="acts%d" % m) for m in range(BLOCKS - 1)]
 
-        for m in range(BLOCKS):
-            result = keep.tile([P, S], F32, name="result%d" % m, tag="slot%d" % m, align_bytes=64)
-            store_cols = S // 2 if m == BLOCKS - 1 else S
-            for j in range(CHUNKS):
-                cols = slice(j * NT, (j + 1) * NT)
-                nc.vector.tensor_tensor(result[:, cols], gates[m][:].indirect(lists[j]), acts[m][:, cols], MULT)
-                done = (j + 1) * NT
-                if done % store_cols == 0:
-                    nc.sync.dma_start(
-                        out=out[m * P : (m + 1) * P, done - store_cols : done],
-                        in_=result[:, done - store_cols : done],
-                    )
+        def project(m, j, c_codes, c_plane):
+            rows = slice(m * P, (m + 1) * P)
+            cols = slice(j * NT, (j + 1) * NT)
+            acc = psum.tile([P, NT], F32, name="acc")
+            nc.tensor.matmul_mx(
+                out=acc[:],
+                lhsT=w4_codes[:, 2 * m * P : 2 * (m + 1) * P].bitcast(FP4X4),
+                lhsT_scale=w4_plane[:, rows],
+                rhs=v_codes[:, cols].bitcast(FP8X4),
+                rhs_scale=v_plane[:, cols],
+                start=True,
+                stop=False,
+            )
+            nc.tensor.matmul_mx(
+                out=acc[:],
+                lhsT=u_codes[:, rows].bitcast(FP8X4),
+                lhsT_scale=u_plane[:, rows],
+                rhs=c_codes[:].bitcast(FP8X4),
+                rhs_scale=c_plane[:],
+                start=False,
+                stop=True,
+            )
+            nc.scalar.activation(acts[m][:, cols], acc[:], GELU, bias=b_cols[:, 32 * m : 32 * m + 1])
+
+        def store(m, first, width, tile):
+            nc.sync.dma_start(out=out[m * P : (m + 1) * P, first : first + width], in_=tile)
+
+        def gate_early(m, j, result):
+            cols = slice(j * NT, (j + 1) * NT)
+            nc.vector.tensor_tensor(result[:, cols], picked[m][:, cols], acts[m][:, cols], MULT)
+
+        def gate_late(m, first, width, result):
+            nc.vector.tensor_tensor(
+                result,
+                gates[m][:].indirect(offsets[:, first // 16 : (first + width) // 16]),
+                acts[m][:, first : first + width],
+                MULT,
+            )
+
+        operands = {}
+        for group in ((0,), (1, 2), (3,)):
+            for j in group:
+                if j == CHUNKS - 1:
+                    grouped = keep.tile([P, NT, PACK], BF16, name="last_grouped", tag="late", align_bytes=64)
+                else:
+                    grouped = ring.tile([P, NT, PACK], BF16, name="grouped", align_bytes=64)
+                operands[j] = quantise(c_raw[j], "c%d" % j, grouped, "c%d_codes" % j)
+            for pair in ((0, 1), (2,)):
+                for j in group:
+                    for m in pair:
+                        project(m, j, *operands[j])
+            if group[0] == 0:
+                nc.vector.tensor_copy(picked[1][:], gates[1][:].indirect(offsets[:]))
+
+        acts.append(keep.tile([P, S], F32, name="c_raw3"))
+        for j in range(CHUNKS):
+            project(BLOCKS - 1, j, *operands[j])
+
+        early = [keep.tile([P, S], F32, name="gates1"), picked[1]]
+        for j in range(CHUNKS - 1):
+            for m in range(EARLY):
+                gate_early(m, j, early[m])
+        for m in range(EARLY):
+            store(m, 0, S - NT, early[m][:, 0 : S - NT])
+        front = keep.tile([P, S // 2], F32, name="front")
+        back = keep.tile([P, S // 2], F32, name="back", tag="late", align_bytes=64)
+        for j in range(2):
+            gate_late(2, j * NT, NT, front[:, j * NT : (j + 1) * NT])
+        store(2, 0, S // 2, front[:])
+        gate_late(2, 2 * NT, NT, back[:, 0:NT])
+        for m in range(EARLY):
+            gate_early(m, CHUNKS - 1, early[m])
+            store(m, S - NT, NT, early[m][:, S - NT : S])
+        gate_late(2, 3 * NT, NT, back[:, NT : 2 * NT])
+        store(2, S // 2, S // 2, back[:])
+        last = keep.tile([P, S], F32, name="last")
+        for first, width in ((0, NT), (NT, NT), (2 * NT, NT), (3 * NT, NT // 2), (3 * NT + NT // 2, NT // 2)):
+            gate_late(3, first, width, last[:, first : first + width])
+            store(3, first, width, last[:, first : first + width])

@@ -26,8 +26,8 @@ EARLY = 2
 
 
 def load_scale_rows(nc, plane, rows):
-    for q in range(4):
-        nc.sync.dma_start(out=plane[32 * q : 32 * q + 4, :].bitcast(I32), in_=rows[4 * q : 4 * q + 4, :].bitcast(I32))
+    for r in range(4):
+        nc.sync.dma_start(out=plane[r:P:32, :].bitcast(I32), in_=rows[r:16:4, :].bitcast(I32))
 
 
 def interleave(copy, grouped, raw):

from contextlib import ExitStack

import concourse.mybir as mybir

K, M, T, S = 512, 512, 4096, 2048
FLOPS = 2 * 2 * K * M * S

F32 = mybir.dt.float32
BF16 = mybir.dt.bfloat16
I32 = mybir.dt.int32
U32 = mybir.dt.uint32
U16 = mybir.dt.uint16
U8 = mybir.dt.uint8
FP8X4 = mybir.dt.float8_e4m3fn_x4
FP4X4 = mybir.dt.float4_e2m1fn_x4
GELU = mybir.ActivationFunctionType.Gelu_apprx_tanh
MULT = mybir.AluOpType.mult

P = 128
PACK = 4
NT = 512
CHUNKS = S // NT
BLOCKS = M // P
LIST_COLS = NT // 16
EARLY = 2


def load_scale_rows(nc, plane, rows):
    for r in range(4):
        nc.sync.dma_start(out=plane[r:P:32, :].bitcast(I32), in_=rows[r:16:4, :].bitcast(I32))


def interleave(copy, grouped, raw):
    copy(
        out=grouped[:].rearrange("p (c i) t -> p c t i", i=4),
        in_=raw.rearrange("p t (c i) -> p c t i", i=4),
    )


def tile_list_tabgate_gelu_kernel(
    tc, tab_words, tab_scales, w4_words, w4_scales, c, u, gT, b, offs, out
):
    nc = tc.nc
    with ExitStack() as ctx:
        keep = ctx.enter_context(tc.tile_pool(name="keep", bufs=1))
        ring = ctx.enter_context(tc.tile_pool(name="ring", bufs=3))
        psum = ctx.enter_context(tc.psum_pool(name="psum", bufs=8))

        offsets = keep.tile([P, S // 16], U16, name="offsets")
        u_raw = keep.tile([P, PACK, M], F32, name="u_raw")
        tab_plane = keep.tile([P, T], U8, name="tab_plane", tag="plane_then_u", align_bytes=64)
        tab_codes = keep.tile([P, T], I32, name="tab_codes", align_bytes=64)
        c_raw = [keep.tile([P, PACK, NT], F32, name="c_raw%d" % j) for j in range(CHUNKS)]
        w4_codes = keep.tile([P, 2 * M], U8, name="w4_codes", align_bytes=64)
        w4_plane = keep.tile([P, M], U8, name="w4_plane", align_bytes=64)
        b_rows = keep.tile([P, P], F32, name="b_rows", align_bytes=64)
        b_cols = keep.tile([P, P], F32, name="b_cols", align_bytes=64)
        gates = [keep.tile([P, T], F32, name="gates%d" % m) for m in range(BLOCKS)]

        nc.vector.memset(tab_plane[:].bitcast(I32), 0)
        nc.vector.memset(w4_plane[:].bitcast(I32), 0)
        nc.vector.memset(b_rows[:], 0.0)

        c_view = c.rearrange("(p t) j -> p t j", t=PACK)

        def load_c(j):
            nc.sync.dma_start(out=c_raw[j][:], in_=c_view[:, :, j * NT : (j + 1) * NT])

        def load_gates(m):
            nc.sync.dma_start(out=gates[m][:], in_=gT[m * P : (m + 1) * P, :])

        nc.sync.dma_start(offsets[:], offs)
        nc.sync.dma_start(out=w4_codes[:].bitcast(I32), in_=w4_words[0].bitcast(I32))
        nc.sync.dma_start(out=u_raw[:], in_=u.rearrange("(p t) n -> p t n", t=PACK))
        load_scale_rows(nc, tab_plane, tab_scales[0])
        nc.sync.dma_start(out=tab_codes[:], in_=tab_words[0].rearrange("p t i -> p (t i)").bitcast(I32))
        load_gates(0)
        load_scale_rows(nc, w4_plane, w4_scales[0])
        nc.sync.dma_start(
            out=b_rows[0:P:32, :].rearrange("q (m r) -> q m r", r=32),
            in_=b.rearrange("(m q r) -> q m r", q=4, r=32),
        )
        load_c(0)
        load_gates(1)
        load_c(1)
        load_c(2)
        load_gates(2)
        load_c(3)
        load_gates(3)

        v_plane = keep.tile([P, S], U8, name="v_plane", align_bytes=64)
        v_codes = keep.tile([P, S], U32, name="v_codes", align_bytes=64)
        nc.vector.tensor_copy(v_plane[:], tab_plane[:].indirect(offsets[:]))
        nc.vector.tensor_copy(v_codes[:], tab_codes[:].bitcast(U32).indirect(offsets[:]))
        picked = [keep.tile([P, S], F32, name="picked%d" % m) for m in range(EARLY)]
        nc.vector.tensor_copy(picked[0][:], gates[0][:].indirect(offsets[:]))

        def quantise(raw, name, grouped, tag):
            interleave(nc.scalar.copy, grouped, raw[:])
            codes = keep.tile([P, NT], U32, name=name + "_codes", tag=tag, align_bytes=64)
            plane = keep.tile([P, NT], U8, name=name + "_plane", align_bytes=64)
            nc.vector.quantize_mx(
                out=codes[:].bitcast(FP8X4), scales=plane[:], in_=grouped[:].rearrange("p w t -> p (w t)")
            )
            return codes, plane

        u_codes, u_plane = quantise(u_raw, "u", ring.tile([P, M, PACK], BF16, name="grouped", align_bytes=64), "plane_then_u")
        nc.vector.transpose(b_cols[:], b_rows[:])

        acts = [keep.tile([P, S], F32, name="acts%d" % m) for m in range(BLOCKS - 1)]

        def project(m, j, c_codes, c_plane):
            rows = slice(m * P, (m + 1) * P)
            cols = slice(j * NT, (j + 1) * NT)
            acc = psum.tile([P, NT], F32, name="acc")
            nc.tensor.matmul_mx(
                out=acc[:],
                lhsT=w4_codes[:, 2 * m * P : 2 * (m + 1) * P].bitcast(FP4X4),
                lhsT_scale=w4_plane[:, rows],
                rhs=v_codes[:, cols].bitcast(FP8X4),
                rhs_scale=v_plane[:, cols],
                start=True,
                stop=False,
            )
            nc.tensor.matmul_mx(
                out=acc[:],
                lhsT=u_codes[:, rows].bitcast(FP8X4),
                lhsT_scale=u_plane[:, rows],
                rhs=c_codes[:].bitcast(FP8X4),
                rhs_scale=c_plane[:],
                start=False,
                stop=True,
            )
            nc.scalar.activation(acts[m][:, cols], acc[:], GELU, bias=b_cols[:, 32 * m : 32 * m + 1])

        def store(m, first, width, tile):
            nc.sync.dma_start(out=out[m * P : (m + 1) * P, first : first + width], in_=tile)

        def gate_early(m, j, result):
            cols = slice(j * NT, (j + 1) * NT)
            nc.vector.tensor_tensor(result[:, cols], picked[m][:, cols], acts[m][:, cols], MULT)

        def gate_late(m, first, width, result):
            nc.vector.tensor_tensor(
                result,
                gates[m][:].indirect(offsets[:, first // 16 : (first + width) // 16]),
                acts[m][:, first : first + width],
                MULT,
            )

        operands = {}
        for group in ((0,), (1, 2), (3,)):
            for j in group:
                if j == CHUNKS - 1:
                    grouped = keep.tile([P, NT, PACK], BF16, name="last_grouped", tag="late", align_bytes=64)
                else:
                    grouped = ring.tile([P, NT, PACK], BF16, name="grouped", align_bytes=64)
                operands[j] = quantise(c_raw[j], "c%d" % j, grouped, "c%d_codes" % j)
            for pair in ((0, 1), (2,)):
                for j in group:
                    for m in pair:
                        project(m, j, *operands[j])
            if group[0] == 0:
                nc.vector.tensor_copy(picked[1][:], gates[1][:].indirect(offsets[:]))

        acts.append(keep.tile([P, S], F32, name="c_raw3"))
        for j in range(CHUNKS):
            project(BLOCKS - 1, j, *operands[j])

        early = [keep.tile([P, S], F32, name="gates1"), picked[1]]
        for j in range(CHUNKS - 1):
            for m in range(EARLY):
                gate_early(m, j, early[m])
        for m in range(EARLY):
            store(m, 0, S - NT, early[m][:, 0 : S - NT])
        front = keep.tile([P, S // 2], F32, name="front")
        back = keep.tile([P, S // 2], F32, name="back", tag="late", align_bytes=64)
        for j in range(2):
            gate_late(2, j * NT, NT, front[:, j * NT : (j + 1) * NT])
        store(2, 0, S // 2, front[:])
        gate_late(2, 2 * NT, NT, back[:, 0:NT])
        for m in range(EARLY):
            gate_early(m, CHUNKS - 1, early[m])
            store(m, S - NT, NT, early[m][:, S - NT : S])
        gate_late(2, 3 * NT, NT, back[:, NT : 2 * NT])
        store(2, S // 2, S // 2, back[:])
        last = keep.tile([P, S], F32, name="last")
        for first, width in ((0, NT), (NT, NT), (2 * NT, NT), (3 * NT, NT // 2), (3 * NT + NT // 2, NT // 2)):
            gate_late(3, first, width, last[:, first : first + width])
            store(3, first, width, last[:, first : first + width])
